import numpy as np
import ml_dtypes


def mxq(x, axis, fmt="e4m3"):
    dtype, down = {"e4m3": (ml_dtypes.float8_e4m3fn, 7), "e5m2": (ml_dtypes.float8_e5m2, 14)}[fmt]
    v = np.moveaxis(np.asarray(x, np.float32).astype(ml_dtypes.bfloat16).astype(np.float64), axis, -1)
    blocks = v.reshape(v.shape[:-1] + (-1, 32))
    amax = np.abs(blocks).max(-1, keepdims=True)
    byte = np.maximum(np.where(amax > 0, np.frexp(amax)[1] - 1 + 127, 0) - down, 1)
    scale = np.exp2(byte - 127.0)
    codes = (blocks / scale).astype(np.float32).astype(dtype).astype(np.float64)
    return np.moveaxis((codes * scale).reshape(v.shape), -1, axis)


WIDE = False


def mx_kscale(k):
    if not WIDE:
        return np.ones(k)
    levels = np.array([10, -10, 5, -5, 0])
    if k % 512:
        return np.exp2(np.random.permutation(np.resize(levels, k // 32))).repeat(32)
    a = np.empty((k // 512, 16))
    for p in range(k // 512):
        a[p, :8] = np.random.permutation(np.resize(levels, 8))
        for g in range(8):
            far = levels[np.abs(levels - a[p, g]) >= 10]
            a[p, g + 8] = far[np.random.randint(len(far))]
    return np.exp2(a.ravel()).repeat(32)


def f64(x):
    return np.asarray(x).astype(np.float64)


def striped(idx):
    return np.tile(np.asarray(idx).reshape(-1, 16).T, (8, 1)).astype(np.uint16)


def unstriped(offs):
    return offs[:16].T.reshape(-1).astype(np.int64)


E2M1 = np.array([0.0, 0.5, 1.0, 1.5, 2.0, 3.0, 4.0, 6.0, -0.0, -0.5, -1.0, -1.5, -2.0, -3.0, -4.0, -6.0])


def pack_weight(w, fmt):
    k, n = w.shape
    w = f64(np.asarray(w, np.float32).astype(ml_dtypes.bfloat16)).reshape(k // 32, 32, n)
    amax = np.abs(w).max(1)
    if fmt == "e4m3":
        byte = np.frexp(amax)[1] - 1 + 127 - 7
    else:
        mant, ex = np.frexp(amax / 6.0)
        byte = np.where(mant > 0.5, ex, ex - 1) + 127
    byte = np.clip(np.where(amax > 0, byte, 1), 1, 254)
    scaled = (w * np.exp2(127.0 - byte)[:, None, :]).reshape(k, n).astype(np.float32)
    by_word = np.ascontiguousarray(scaled.reshape(k // 512, 128, 4, n).transpose(0, 1, 3, 2))
    if fmt == "e4m3":
        words = by_word.astype(ml_dtypes.float8_e4m3fn).view(np.uint8)
    else:
        c = by_word.astype(ml_dtypes.float4_e2m1fn).view(np.uint8) & 0xF
        words = (c[..., 0::2] | (c[..., 1::2] << 4)).reshape(k // 512, 128, 2 * n)
    return np.ascontiguousarray(words), np.ascontiguousarray(byte.astype(np.uint8).reshape(k // 512, 16, n))


def unpack_weight(words, scales, fmt):
    g, _, n = scales.shape
    words = np.ascontiguousarray(words).reshape(g, 128, n, -1)
    if fmt == "e4m3":
        vals = words.view(ml_dtypes.float8_e4m3fn).astype(np.float64)
    else:
        nib = np.empty((g, 128, n, 4), np.uint8)
        nib[..., 0::2] = words & 0xF
        nib[..., 1::2] = words >> 4
        vals = E2M1[nib]
    vals = vals * np.repeat(np.exp2(scales.astype(np.float64) - 127.0), 8, axis=1)[..., None]
    return vals.transpose(0, 1, 3, 2).reshape(g * 512, n)


D, T, I, J, U, Z, E, Y = 512, 2048, 512, 512, 1024, 1024, 512, 1024


def setup_inputs():
    n = np.random.standard_normal
    idx = np.random.permutation(T)[:I]
    idx2 = np.random.permutation(U)[:J]
    idx3 = np.random.permutation(Z)[:J]
    idx4 = np.random.permutation(Y)[:I]
    fd = mx_kscale(D)
    fi = mx_kscale(I)
    ti = np.ones(T)
    ti[idx] = fi
    ti4 = np.ones(Y)
    ti4[idx4] = fi
    keysp = pack_weight(n((D, T)) / fd[:, None], "e4m3")
    return {
        "keys_words": keysp[0],
        "keys_scales": keysp[1],
        "notes": (n((D, U)) * 1.0 / np.sqrt(D) * fd[:, None]).astype(np.float32),
        "given": (np.random.uniform(0.3, 1.7, (I, Z))).astype(np.float32),
        "rowf": (np.random.uniform(0.02, 0.08, (I, 1)) * fi[:, None]).astype(np.float32),
        "rowf2": (np.random.uniform(0.02, 0.08, (I, 1)) * fi[:, None]).astype(np.float32),
        "vals": (n((E, T)) / ti).astype(np.float32),
        "vals2": (n((E, Y)) / ti4).astype(np.float32),
        "offs": striped(idx),
        "offs2": striped(idx2),
        "offs3": striped(idx3),
        "offs4": striped(idx4),
    }


def reference(keys_words, keys_scales, notes, given, rowf, rowf2, vals, vals2, offs, offs2, offs3, offs4):
    idx = unstriped(offs)
    idx2 = unstriped(offs2)
    idx3 = unstriped(offs3)
    idx4 = unstriped(offs4)
    keysu = unpack_weight(keys_words, keys_scales, "e4m3")
    keysidxg = keysu[:, idx]
    notesidx2q = mxq(f64(notes)[:, idx2], 0, "e4m3")
    g1 = keysidxg.T @ notesidx2q
    g0 = g1 * f64(given)[:, idx3]
    gr1 = g0 * f64(rowf)
    gr2 = g0 * f64(rowf2)
    vt1 = f64(vals)[:, idx].T
    vt2 = f64(vals2)[:, idx4].T
    vt1q = mxq(vt1, 0, "e4m3")
    gr1q = mxq(gr1, 0, "e4m3")
    vt2q = mxq(vt2, 0, "e4m3")
    gr2q = mxq(gr2, 0, "e4m3")
    o = vt1q.T @ gr1q + vt2q.T @ gr2q
    return o

@@ -1,0 +1,193 @@
+from contextlib import ExitStack
+
+import concourse.mybir as mybir
+from concourse.masks import make_identity
+
+D, T, I, J, U, Z, E, Y = 512, 2048, 512, 512, 1024, 1024, 512, 1024
+FLOPS = 2 * D * I * J + 2 * 2 * I * E * J
+
+F32 = mybir.dt.float32
+BF16 = mybir.dt.bfloat16
+I32 = mybir.dt.int32
+U32 = mybir.dt.uint32
+U16 = mybir.dt.uint16
+U8 = mybir.dt.uint8
+FP8X4 = mybir.dt.float8_e4m3fn_x4
+MULT = mybir.AluOpType.mult
+COPY = mybir.ActivationFunctionType.Copy
+
+P = 128
+PACK = 4
+BLOCKS = E // P
+
+
+def tile_attend_tab_timestable_twostores_kernel(
+    tc, keys_words, keys_scales, notes, given, rowf, rowf2, vals, vals2, offs, offs2, offs3, offs4, out
+):
+    nc = tc.nc
+    with ExitStack() as ctx:
+        held = ctx.enter_context(tc.tile_pool(name="held", bufs=1))
+        banks = ctx.enter_context(tc.psum_pool(name="banks", bufs=1))
+        turns = ctx.enter_context(tc.psum_pool(name="turns", bufs=4))
+
+        def load_list(src, name):
+            t = held.tile([P, I // 16], U16, name=name)
+            nc.sync.dma_start(t[:], src)
+            return t
+
+        def load(src, width, dtype, name):
+            t = held.tile([P, width], dtype, name=name)
+            nc.sync.dma_start(out=t[:], in_=src)
+            return t
+
+        def gather(on_scalar, dst, window, offsets):
+            if on_scalar:
+                nc.scalar.activation(dst, window[:].indirect(offsets), COPY)
+            else:
+                nc.vector.tensor_copy(dst, window[:].indirect(offsets))
+
+        def interleave(planes, name):
+            woven = held.tile([P, J, PACK], BF16, name=name, align_bytes=64)
+            nc.vector.tensor_copy(
+                out=woven[:].rearrange("p (c n) t -> p c t n", n=4),
+                in_=planes[:].rearrange("p t (c n) -> p c t n", n=4),
+            )
+            return woven[:].rearrange("p j t -> p (j t)")
+
+        def quantize(src, width, name):
+            codes = held.tile([P, width], U32, name=name + "_codes", align_bytes=64)
+            scales = held.tile([P, width], U8, name=name + "_scales", align_bytes=64)
+            nc.vector.quantize_mx(out=codes[:].bitcast(FP8X4), scales=scales[:], in_=src)
+            return codes, scales
+
+        key_scales = held.tile([P, T], U8, name="key_scales")
+        nc.vector.memset(key_scales[:].bitcast(I32), 0)
+        factors = []
+        for s, src in enumerate((rowf, rowf2)):
+            t = held.tile([P, PACK], F32, name="factor%d" % s)
+            nc.gpsimd.dma_start(out=t[:], in_=src.rearrange("(p t) o -> p (t o)", t=PACK))
+            factors.append(t)
+        ident = held.tile([P, P], F32, name="ident")
+        make_identity(nc, ident[:])
+
+        notes_rows = notes.rearrange("(p t) u -> p t u", t=PACK)
+        given_rows = given.rearrange("(p t) z -> p t z", t=PACK)
+        def load_scale_rows(q):
+            nc.sync.dma_start(
+                out=key_scales[32 * q : 32 * q + 4, :].bitcast(I32),
+                in_=keys_scales[0, 4 * q : 4 * q + 4, :].bitcast(I32),
+            )
+
+        list1 = load_list(offs, "list1")
+        key_words = load(keys_words[0].rearrange("p n t -> p (n t)").bitcast(I32), T, I32, "key_words")
+        list2 = load_list(offs2, "list2")
+        note_pool = [load(notes_rows[:, t, :], U, F32, "notes%d" % t) for t in range(2)]
+        load_scale_rows(0)
+        load_scale_rows(1)
+        note_pool.append(load(notes_rows[:, 2, :], U, F32, "notes2"))
+        load_scale_rows(2)
+        load_scale_rows(3)
+        note_pool.append(load(notes_rows[:, 3, :], U, F32, "notes3"))
+        given_pool = [load(given_rows[:, 0, :], Z, F32, "given0")]
+        list3 = load_list(offs3, "list3")
+        for t in range(1, PACK):
+            given_pool.append(load(given_rows[:, t, :], Z, F32, "given%d" % t))
+        list4 = load_list(offs4, "list4")
+        second_pool = [load(vals2[P * b : P * (b + 1), :], Y, F32, "vals2_%d" % b) for b in range(BLOCKS)]
+        first_pool = [load(vals[P * b : P * (b + 1), :], T, F32, "vals_%d" % b) for b in range(BLOCKS)]
+
+        def gather_halves(dst, window, offsets):
+            gather(False, dst[:, 0:256], window, offsets[:, 0:16])
+            gather(True, dst[:, 256:512], window, offsets[:, 16:32])
+
+        picked_words = held.tile([P, I], U32, name="picked_words", align_bytes=64)
+        nc.vector.tensor_copy(
+            picked_words[:].rearrange("p (r s) -> p s r", r=PACK), key_words[:].bitcast(U32).indirect(list1[:])
+        )
+        picked_scales = held.tile([P, I], U8, name="picked_scales", align_bytes=64)
+        nc.vector.tensor_copy(
+            picked_scales[:].rearrange("p (r s) -> p s r", r=PACK), key_scales[:].indirect(list1[:])
+        )
+
+        note_planes = held.tile([P, PACK, J], BF16, name="note_planes")
+        gather(True, note_planes[:, 0, :], note_pool[0], list2[:])
+        gather(True, note_planes[:, 1, :], note_pool[1], list2[:])
+        gather(False, note_planes[:, 2, :], note_pool[2], list2[:])
+        gather_halves(note_planes[:, 3, :], note_pool[3], list2)
+        note_codes, note_scales = quantize(interleave(note_planes, "note_woven"), J, "note")
+
+        table_planes = [held.tile([P, PACK, J], BF16, name="table_planes%d" % s) for s in range(2)]
+        for r in range(PACK):
+            cols = slice(P * r, P * (r + 1))
+            g1 = banks.tile([P, J], F32, name="g1_%d" % r, tag="bank%d" % r)
+            nc.tensor.matmul_mx(
+                out=g1[:],
+                lhsT=picked_words[:, cols].bitcast(FP8X4),
+                lhsT_scale=picked_scales[:, cols],
+                rhs=note_codes[:].bitcast(FP8X4),
+                rhs_scale=note_scales[:],
+                start=True,
+                stop=True,
+            )
+            picked_given = held.tile([P, J], F32, name="picked_given%d" % r)
+            gather(True, picked_given[:], given_pool[r], list3[:])
+            for s in range(2):
+                nc.vector.scalar_tensor_tensor(
+                    out=table_planes[s][:, r, :],
+                    in0=g1[:],
+                    scalar=factors[s][:, r : r + 1],
+                    in1=picked_given[:],
+                    op0=MULT,
+                    op1=MULT,
+                )
+        tables = [quantize(interleave(table_planes[s], "table_woven%d" % s), J, "table%d" % s) for s in range(2)]
+
+        def turn_and_quantize(picked, copy_on_scalar, name):
+            words = picked[:].bitcast(F32)
+            turned = turns.tile([P, 2, P], F32, name="turned")
+            for u in range(2):
+                nc.tensor.transpose(turned[:, u, :], words[:, u : I // 2 : 2], ident[:])
+            woven = held.tile([P, P * PACK], BF16, name=name + "_woven", align_bytes=64)
+            dst = woven[:].bitcast(F32).rearrange("p (e u) -> p e u", u=2)
+            src = turned[:].rearrange("p u e -> p e u")
+            if copy_on_scalar:
+                nc.scalar.copy(out=dst, in_=src)
+            else:
+                nc.vector.tensor_copy(out=dst, in_=src)
+            return quantize(woven[:], P, name)
+
+        second = []
+        for b in range(BLOCKS):
+            picked = held.tile([P, I], BF16, name="picked2_%d" % b)
+            gather(True, picked[:], second_pool[b], list4[:])
+            second.append(turn_and_quantize(picked, False, "second%d" % b))
+
+        for b in range(BLOCKS):
+            last = b == BLOCKS - 1
+            picked = held.tile([P, I], BF16, name="picked1_%d" % b)
+            if last:
+                gather_halves(picked[:], first_pool[b], list1)
+            else:
+                gather(True, picked[:], first_pool[b], list1[:])
+            first = turn_and_quantize(picked, True, "first%d" % b)
+            pieces = 2 if last else 1
+            width = J // pieces
+            for h in range(pieces):
+                cols = slice(width * h, width * (h + 1))
+                acc = banks.tile([P, width], F32, name="acc%d_%d" % (b, h), tag="bank%d" % ((b + h) % PACK))
+                for n, (stat, table) in enumerate(((second[b], tables[1]), (first, tables[0]))):
+                    nc.tensor.matmul_mx(
+                        out=acc[:],
+                        lhsT=stat[0][:].bitcast(FP8X4),
+                        lhsT_scale=stat[1][:],
+                        rhs=table[0][:, cols].bitcast(FP8X4),
+                        rhs_scale=table[1][:, cols],
+                        start=(n == 0),
+                        stop=(n == 1),
+                    )
+                result = held.tile([P, width], F32, name="result%d_%d" % (b, h))
+                if h == 1:
+                    nc.scalar.copy(out=result[:], in_=acc[:])
+                else:
+                    nc.vector.tensor_copy(out=result[:], in_=acc[:])
+                nc.sync.dma_start(out=out[P * b : P * (b + 1), cols], in_=result[:])

@@ -28,7 +28,6 @@ def tile_attend_tab_timestable_twostores_kernel(
     with ExitStack() as ctx:
         held = ctx.enter_context(tc.tile_pool(name="held", bufs=1))
         banks = ctx.enter_context(tc.psum_pool(name="banks", bufs=1))
-        turns = ctx.enter_context(tc.psum_pool(name="turns", bufs=4))
 
         def load_list(src, name):
             t = held.tile([P, I // 16], U16, name=name)
@@ -36,7 +35,7 @@ def tile_attend_tab_timestable_twostores_kernel(
             return t
 
         def load(src, width, dtype, name):
-            t = held.tile([P, width], dtype, name=name)
+            t = held.tile([P, width], dtype, name=name, align_bytes=64)
             nc.sync.dma_start(out=t[:], in_=src)
             return t
 
@@ -46,16 +45,21 @@ def tile_attend_tab_timestable_twostores_kernel(
             else:
                 nc.vector.tensor_copy(dst, window[:].indirect(offsets))
 
-        def interleave(planes, name):
+        def interleave(planes, name, cut=0):
             woven = held.tile([P, J, PACK], BF16, name=name, align_bytes=64)
+            if cut > 0:
+                nc.scalar.copy(
+                    out=woven[:, 0:cut, :].rearrange("p (c n) t -> p c t n", n=4),
+                    in_=planes[:, :, 0:cut].rearrange("p t (c n) -> p c t n", n=4),
+                )
             nc.vector.tensor_copy(
-                out=woven[:].rearrange("p (c n) t -> p c t n", n=4),
-                in_=planes[:].rearrange("p t (c n) -> p c t n", n=4),
+                out=woven[:, cut:J, :].rearrange("p (c n) t -> p c t n", n=4),
+                in_=planes[:, :, cut:J].rearrange("p t (c n) -> p c t n", n=4),
             )
             return woven[:].rearrange("p j t -> p (j t)")
 
-        def quantize(src, width, name):
-            codes = held.tile([P, width], U32, name=name + "_codes", align_bytes=64)
+        def quantize(src, width, name, tag=None):
+            codes = held.tile([P, width], U32, name=name + "_codes", tag=tag or name + "_codes", align_bytes=64)
             scales = held.tile([P, width], U8, name=name + "_scales", align_bytes=64)
             nc.vector.quantize_mx(out=codes[:].bitcast(FP8X4), scales=scales[:], in_=src)
             return codes, scales
@@ -72,49 +76,52 @@ def tile_attend_tab_timestable_twostores_kernel(
 
         notes_rows = notes.rearrange("(p t) u -> p t u", t=PACK)
         given_rows = given.rearrange("(p t) z -> p t z", t=PACK)
-        def load_scale_rows(q):
+        lists = {}
+        note_pool = []
+        for t, (name, src) in enumerate((("list2", offs2), ("list1", offs), ("list3", offs3), ("list4", offs4))):
+            lists[name] = load_list(src, name)
+            note_pool.append(load(notes_rows[:, t, :], U, F32, "notes%d" % t))
+        list1, list2, list3, list4 = lists["list1"], lists["list2"], lists["list3"], lists["list4"]
+        for q in range(4):
             nc.sync.dma_start(
                 out=key_scales[32 * q : 32 * q + 4, :].bitcast(I32),
                 in_=keys_scales[0, 4 * q : 4 * q + 4, :].bitcast(I32),
             )
+        def load_second(b):
+            return load(vals2[P * b : P * (b + 1), :], Y, F32, "vals2_%d" % b)
 
-        list1 = load_list(offs, "list1")
+        EARLY = 0
+        second_pool = [load_second(b) for b in range(EARLY)]
         key_words = load(keys_words[0].rearrange("p n t -> p (n t)").bitcast(I32), T, I32, "key_words")
-        list2 = load_list(offs2, "list2")
-        note_pool = [load(notes_rows[:, t, :], U, F32, "notes%d" % t) for t in range(2)]
-        load_scale_rows(0)
-        load_scale_rows(1)
-        note_pool.append(load(notes_rows[:, 2, :], U, F32, "notes2"))
-        load_scale_rows(2)
-        load_scale_rows(3)
-        note_pool.append(load(notes_rows[:, 3, :], U, F32, "notes3"))
-        given_pool = [load(given_rows[:, 0, :], Z, F32, "given0")]
-        list3 = load_list(offs3, "list3")
-        for t in range(1, PACK):
-            given_pool.append(load(given_rows[:, t, :], Z, F32, "given%d" % t))
-        list4 = load_list(offs4, "list4")
-        second_pool = [load(vals2[P * b : P * (b + 1), :], Y, F32, "vals2_%d" % b) for b in range(BLOCKS)]
+        given_pool = [load(given_rows[:, t, :], Z, F32, "given%d" % t) for t in range(PACK)]
+        second_pool.extend(load_second(b) for b in range(EARLY, BLOCKS))
         first_pool = [load(vals[P * b : P * (b + 1), :], T, F32, "vals_%d" % b) for b in range(BLOCKS)]
 
-        def gather_halves(dst, window, offsets):
-            gather(False, dst[:, 0:256], window, offsets[:, 0:16])
-            gather(True, dst[:, 256:512], window, offsets[:, 16:32])
+        def gather_split(dst, window, offsets, cut):
+            if cut > 0:
+                gather(True, dst[:, 0:cut], window, offsets[:, 0 : cut // 16])
+            if cut < I:
+                gather(False, dst[:, cut:I], window, offsets[:, cut // 16 : I // 16])
 
-        picked_words = held.tile([P, I], U32, name="picked_words", align_bytes=64)
-        nc.vector.tensor_copy(
-            picked_words[:].rearrange("p (r s) -> p s r", r=PACK), key_words[:].bitcast(U32).indirect(list1[:])
-        )
+        def copy_out(on_scalar, dst, src):
+            if on_scalar:
+                nc.scalar.copy(out=dst, in_=src)
+            else:
+                nc.vector.tensor_copy(out=dst, in_=src)
+
+        note_planes = held.tile([P, PACK, J], BF16, name="note_planes")
+        NOTE_S = (512,0,0,256)
+        for t in range(PACK):
+            gather_split(note_planes[:, t, :], note_pool[t], list2, NOTE_S[t])
         picked_scales = held.tile([P, I], U8, name="picked_scales", align_bytes=64)
         nc.vector.tensor_copy(
             picked_scales[:].rearrange("p (r s) -> p s r", r=PACK), key_scales[:].indirect(list1[:])
         )
-
-        note_planes = held.tile([P, PACK, J], BF16, name="note_planes")
-        gather(True, note_planes[:, 0, :], note_pool[0], list2[:])
-        gather(True, note_planes[:, 1, :], note_pool[1], list2[:])
-        gather(False, note_planes[:, 2, :], note_pool[2], list2[:])
-        gather_halves(note_planes[:, 3, :], note_pool[3], list2)
-        note_codes, note_scales = quantize(interleave(note_planes, "note_woven"), J, "note")
+        note_codes, note_scales = quantize(interleave(note_planes, "note_woven", 256), J, "note")
+        picked_words = held.tile([P, I], U32, name="picked_words", align_bytes=64)
+        nc.vector.tensor_copy(
+            picked_words[:].rearrange("p (r s) -> p s r", r=PACK), key_words[:].bitcast(U32).indirect(list1[:])
+        )
 
         table_planes = [held.tile([P, PACK, J], BF16, name="table_planes%d" % s) for s in range(2)]
         for r in range(PACK):
@@ -130,7 +137,7 @@ def tile_attend_tab_timestable_twostores_kernel(
                 stop=True,
             )
             picked_given = held.tile([P, J], F32, name="picked_given%d" % r)
-            gather(True, picked_given[:], given_pool[r], list3[:])
+            gather_split(picked_given[:], given_pool[r], list3, (512,512,512,512)[r])
             for s in range(2):
                 nc.vector.scalar_tensor_tensor(
                     out=table_planes[s][:, r, :],
@@ -142,52 +149,68 @@ def tile_attend_tab_timestable_twostores_kernel(
                 )
         tables = [quantize(interleave(table_planes[s], "table_woven%d" % s), J, "table%d" % s) for s in range(2)]
 
-        def turn_and_quantize(picked, copy_on_scalar, name):
+        def turn(picked, turned):
             words = picked[:].bitcast(F32)
-            turned = turns.tile([P, 2, P], F32, name="turned")
             for u in range(2):
                 nc.tensor.transpose(turned[:, u, :], words[:, u : I // 2 : 2], ident[:])
-            woven = held.tile([P, P * PACK], BF16, name=name + "_woven", align_bytes=64)
-            dst = woven[:].bitcast(F32).rearrange("p (e u) -> p e u", u=2)
-            src = turned[:].rearrange("p u e -> p e u")
-            if copy_on_scalar:
-                nc.scalar.copy(out=dst, in_=src)
-            else:
-                nc.vector.tensor_copy(out=dst, in_=src)
-            return quantize(woven[:], P, name)
 
-        second = []
-        for b in range(BLOCKS):
-            picked = held.tile([P, I], BF16, name="picked2_%d" % b)
-            gather(True, picked[:], second_pool[b], list4[:])
-            second.append(turn_and_quantize(picked, False, "second%d" % b))
+        second = {}
 
+        def second_group(blocks, bank, on_scalar):
+            n = len(blocks)
+            woven = held.tile([P, n * P * PACK], BF16, name="second_woven%d" % blocks[0], align_bytes=64)
+            turned = banks.tile([P, n, 2, P], F32, name="turned2_%d" % blocks[0], tag="bank%d" % bank)
+            for k, b in enumerate(blocks):
+                picked = held.tile([P, I], BF16, name="picked2_%d" % b)
+                gather(True, picked[:], second_pool[b], list4[:])
+                turn(picked, turned[:, k])
+            copy_out(
+                on_scalar,
+                woven[:].bitcast(F32).rearrange("p (k e u) -> p k e u", k=n, u=2),
+                turned[:].rearrange("p k u e -> p k e u"),
+            )
+            codes, scales = quantize(woven[:], n * P, "second%d" % blocks[0])
+            for k, b in enumerate(blocks):
+                second[b] = (codes[:, P * k : P * (k + 1)], scales[:, P * k : P * (k + 1)])
+
+        for blocks, bank, on_scalar in (((0,1),4,False),((2,3),5,False)):
+            second_group(blocks, bank, on_scalar)
+
+        SHARE = (512,512,512,512)
+        CV_S = (False,False,False,True)
+        OUT_S = (False,False,True,False,True)
+        TURN_BANK = (6, 7, 0, 1)
         for b in range(BLOCKS):
             last = b == BLOCKS - 1
             picked = held.tile([P, I], BF16, name="picked1_%d" % b)
-            if last:
-                gather_halves(picked[:], first_pool[b], list1)
-            else:
-                gather(True, picked[:], first_pool[b], list1[:])
-            first = turn_and_quantize(picked, True, "first%d" % b)
+            gather_split(picked[:], first_pool[b], list1, SHARE[b])
+            turned = banks.tile([P, 2, P], F32, name="turned1_%d" % b, tag="bank%d" % TURN_BANK[b])
+            turn(picked, turned)
+            woven = held.tile([P, P * PACK], BF16, name="first_woven%d" % b, align_bytes=64)
+            copy_out(
+                CV_S[b],
+                woven[:].bitcast(F32).rearrange("p (e u) -> p e u", u=2),
+                turned[:].rearrange("p u e -> p e u"),
+            )
+            first = quantize(woven[:], P, "first%d" % b, None if last else "vals_%d" % (b + 1))
             pieces = 2 if last else 1
             width = J // pieces
             for h in range(pieces):
                 cols = slice(width * h, width * (h + 1))
-                acc = banks.tile([P, width], F32, name="acc%d_%d" % (b, h), tag="bank%d" % ((b + h) % PACK))
-                for n, (stat, table) in enumerate(((second[b], tables[1]), (first, tables[0]))):
+                acc = banks.tile([P, width], F32, name="acc%d_%d" % (b, h), tag="bank%d" % (TURN_BANK[b] if h == 0 else 6))
+                passes = [(second[b][0], second[b][1], tables[1]), (first[0][:], first[1][:], tables[0])]
+                if h == 1 and False:
+                    passes = passes[::-1]
+                for n, (codes, scales, table) in enumerate(passes):
                     nc.tensor.matmul_mx(
                         out=acc[:],
-                        lhsT=stat[0][:].bitcast(FP8X4),
-                        lhsT_scale=stat[1][:],
+                        lhsT=codes.bitcast(FP8X4),
+                        lhsT_scale=scales,
                         rhs=table[0][:, cols].bitcast(FP8X4),
                         rhs_scale=table[1][:, cols],
                         start=(n == 0),
                         stop=(n == 1),
                     )
-                result = held.tile([P, width], F32, name="result%d_%d" % (b, h))
-                if h == 1:
-                    nc.scalar.copy(out=result[:], in_=acc[:])
-                else:
-                    nc.vector.tensor_copy(out=result[:], in_=acc[:])
+                result = held.tile([P, width], F32, name="result%d_%d" % (b, h), align_bytes=64)
+                copy_out(OUT_S[b + h], result[:], acc[:])
                 nc.sync.dma_start(out=out[P * b : P * (b + 1), cols], in_=result[:])

@@ -65,7 +65,7 @@ def tile_attend_tab_timestable_twostores_kernel(
             return codes, scales
 
         key_scales = held.tile([P, T], U8, name="key_scales")
-        nc.vector.memset(key_scales[:].bitcast(I32), 0)
+        nc.gpsimd.memset(key_scales[:].bitcast(I32), 0)
         factors = []
         for s, src in enumerate((rowf, rowf2)):
             t = held.tile([P, PACK], F32, name="factor%d" % s)
@@ -76,24 +76,27 @@ def tile_attend_tab_timestable_twostores_kernel(
 
         notes_rows = notes.rearrange("(p t) u -> p t u", t=PACK)
         given_rows = given.rearrange("(p t) z -> p t z", t=PACK)
-        lists = {}
-        note_pool = []
-        for t, (name, src) in enumerate((("list2", offs2), ("list1", offs), ("list3", offs3), ("list4", offs4))):
-            lists[name] = load_list(src, name)
-            note_pool.append(load(notes_rows[:, t, :], U, F32, "notes%d" % t))
-        list1, list2, list3, list4 = lists["list1"], lists["list2"], lists["list3"], lists["list4"]
+        list2 = load_list(offs2, "list2")
+        note_pool = [load(notes_rows[:, 0, :], U, F32, "notes0")]
+        list1 = load_list(offs, "list1")
+        note_pool.append(load(notes_rows[:, 1, :], U, F32, "notes1"))
         for q in range(4):
             nc.sync.dma_start(
                 out=key_scales[32 * q : 32 * q + 4, :].bitcast(I32),
                 in_=keys_scales[0, 4 * q : 4 * q + 4, :].bitcast(I32),
             )
+        for t in range(2, PACK):
+            note_pool.append(load(notes_rows[:, t, :], U, F32, "notes%d" % t))
+
         def load_second(b):
             return load(vals2[P * b : P * (b + 1), :], Y, F32, "vals2_%d" % b)
 
         EARLY = 0
         second_pool = [load_second(b) for b in range(EARLY)]
         key_words = load(keys_words[0].rearrange("p n t -> p (n t)").bitcast(I32), T, I32, "key_words")
+        list3 = load_list(offs3, "list3")
         given_pool = [load(given_rows[:, t, :], Z, F32, "given%d" % t) for t in range(PACK)]
+        list4 = load_list(offs4, "list4")
         second_pool.extend(load_second(b) for b in range(EARLY, BLOCKS))
         first_pool = [load(vals[P * b : P * (b + 1), :], T, F32, "vals_%d" % b) for b in range(BLOCKS)]
 
@@ -110,14 +113,14 @@ def tile_attend_tab_timestable_twostores_kernel(
                 nc.vector.tensor_copy(out=dst, in_=src)
 
         note_planes = held.tile([P, PACK, J], BF16, name="note_planes")
-        NOTE_S = (512,0,0,256)
+        NOTE_S = (512,0,512,256)
         for t in range(PACK):
             gather_split(note_planes[:, t, :], note_pool[t], list2, NOTE_S[t])
         picked_scales = held.tile([P, I], U8, name="picked_scales", align_bytes=64)
         nc.vector.tensor_copy(
             picked_scales[:].rearrange("p (r s) -> p s r", r=PACK), key_scales[:].indirect(list1[:])
         )
-        note_codes, note_scales = quantize(interleave(note_planes, "note_woven", 256), J, "note")
+        note_codes, note_scales = quantize(interleave(note_planes, "note_woven", 160), J, "note")
         picked_words = held.tile([P, I], U32, name="picked_words", align_bytes=64)
         nc.vector.tensor_copy(
             picked_words[:].rearrange("p (r s) -> p s r", r=PACK), key_words[:].bitcast(U32).indirect(list1[:])
@@ -137,7 +140,7 @@ def tile_attend_tab_timestable_twostores_kernel(
                 stop=True,
             )
             picked_given = held.tile([P, J], F32, name="picked_given%d" % r)
-            gather_split(picked_given[:], given_pool[r], list3, (512,512,512,512)[r])
+            gather_split(picked_given[:], given_pool[r], list3, (256,512,512,512)[r])
             for s in range(2):
                 nc.vector.scalar_tensor_tensor(
                     out=table_planes[s][:, r, :],
@@ -176,30 +179,32 @@ def tile_attend_tab_timestable_twostores_kernel(
         for blocks, bank, on_scalar in (((0,1),4,False),((2,3),5,False)):
             second_group(blocks, bank, on_scalar)
 
-        SHARE = (512,512,512,512)
+        SHARE = (512,512,512,256)
         CV_S = (False,False,False,True)
         OUT_S = (False,False,True,False,True)
         TURN_BANK = (6, 7, 0, 1)
         for b in range(BLOCKS):
             last = b == BLOCKS - 1
-            picked = held.tile([P, I], BF16, name="picked1_%d" % b)
+            picked = held.tile([P, I], BF16, name="picked1_%d" % b, align_bytes=64)
             gather_split(picked[:], first_pool[b], list1, SHARE[b])
             turned = banks.tile([P, 2, P], F32, name="turned1_%d" % b, tag="bank%d" % TURN_BANK[b])
             turn(picked, turned)
-            woven = held.tile([P, P * PACK], BF16, name="first_woven%d" % b, align_bytes=64)
+            if last:
+                waiting(tag="picked1_%d" % b)
+            woven = held.tile([P, P * PACK], BF16, name="first_woven%d" % b, tag="vals_3" if b == 2 else "first_woven%d" % b, align_bytes=64)
             copy_out(
                 CV_S[b],
                 woven[:].bitcast(F32).rearrange("p (e u) -> p e u", u=2),
                 turned[:].rearrange("p u e -> p e u"),
             )
-            first = quantize(woven[:], P, "first%d" % b, None if last else "vals_%d" % (b + 1))
+            first = quantize(woven[:], P, "first%d" % b, "vals_%d" % (b + 1) if b < 2 else None)
             pieces = 2 if last else 1
             width = J // pieces
             for h in range(pieces):
                 cols = slice(width * h, width * (h + 1))
                 acc = banks.tile([P, width], F32, name="acc%d_%d" % (b, h), tag="bank%d" % (TURN_BANK[b] if h == 0 else 6))
                 passes = [(second[b][0], second[b][1], tables[1]), (first[0][:], first[1][:], tables[0])]
-                if h == 1 and False:
+                if (False,False,False,False,False)[b + h]:
                     passes = passes[::-1]
                 for n, (codes, scales, table) in enumerate(passes):
                     nc.tensor.matmul_mx(
@@ -211,6 +216,12 @@ def tile_attend_tab_timestable_twostores_kernel(
                         start=(n == 0),
                         stop=(n == 1),
                     )
-                result = held.tile([P, width], F32, name="result%d_%d" % (b, h), align_bytes=64)
-                copy_out(OUT_S[b + h], result[:], acc[:])
-                nc.sync.dma_start(out=out[P * b : P * (b + 1), cols], in_=result[:])
+                def leave(b=b, h=h, acc=acc, cols=cols, width=width, tag=None):
+                    result = held.tile([P, width], F32, name="result%d_%d" % (b, h), tag=tag or "result%d_%d" % (b, h), align_bytes=64)
+                    copy_out(OUT_S[b + h], result[:], acc[:])
+                    nc.sync.dma_start(out=out[P * b : P * (b + 1), cols], in_=result[:])
+
+                if b == 1:
+                    waiting = leave
+                else:
+                    leave()

@@ -76,17 +76,22 @@ def tile_attend_tab_timestable_twostores_kernel(
 
         notes_rows = notes.rearrange("(p t) u -> p t u", t=PACK)
         given_rows = given.rearrange("(p t) z -> p t z", t=PACK)
-        list2 = load_list(offs2, "list2")
-        note_pool = [load(notes_rows[:, 0, :], U, F32, "notes0")]
-        list1 = load_list(offs, "list1")
-        note_pool.append(load(notes_rows[:, 1, :], U, F32, "notes1"))
-        for q in range(4):
+        def load_scale_rows(q):
             nc.sync.dma_start(
                 out=key_scales[32 * q : 32 * q + 4, :].bitcast(I32),
                 in_=keys_scales[0, 4 * q : 4 * q + 4, :].bitcast(I32),
             )
-        for t in range(2, PACK):
-            note_pool.append(load(notes_rows[:, t, :], U, F32, "notes%d" % t))
+
+        note_pool = [load(notes_rows[:, 0, :], U, F32, "notes0")]
+        list2 = load_list(offs2, "list2")
+        note_pool.append(load(notes_rows[:, 1, :], U, F32, "notes1"))
+        list1 = load_list(offs, "list1")
+        note_pool.append(load(notes_rows[:, 2, :], U, F32, "notes2"))
+        load_scale_rows(0)
+        load_scale_rows(1)
+        note_pool.append(load(notes_rows[:, 3, :], U, F32, "notes3"))
+        load_scale_rows(2)
+        load_scale_rows(3)
 
         def load_second(b):
             return load(vals2[P * b : P * (b + 1), :], Y, F32, "vals2_%d" % b)
@@ -113,14 +118,14 @@ def tile_attend_tab_timestable_twostores_kernel(
                 nc.vector.tensor_copy(out=dst, in_=src)
 
         note_planes = held.tile([P, PACK, J], BF16, name="note_planes")
-        NOTE_S = (512,0,512,256)
+        NOTE_S = (512,0,0,352)
         for t in range(PACK):
             gather_split(note_planes[:, t, :], note_pool[t], list2, NOTE_S[t])
         picked_scales = held.tile([P, I], U8, name="picked_scales", align_bytes=64)
         nc.vector.tensor_copy(
             picked_scales[:].rearrange("p (r s) -> p s r", r=PACK), key_scales[:].indirect(list1[:])
         )
-        note_codes, note_scales = quantize(interleave(note_planes, "note_woven", 160), J, "note")
+        note_codes, note_scales = quantize(interleave(note_planes, "note_woven", 256), J, "note")
         picked_words = held.tile([P, I], U32, name="picked_words", align_bytes=64)
         nc.vector.tensor_copy(
             picked_words[:].rearrange("p (r s) -> p s r", r=PACK), key_words[:].bitcast(U32).indirect(list1[:])
@@ -179,8 +184,9 @@ def tile_attend_tab_timestable_twostores_kernel(
         for blocks, bank, on_scalar in (((0,1),4,False),((2,3),5,False)):
             second_group(blocks, bank, on_scalar)
 
-        SHARE = (512,512,512,256)
-        CV_S = (False,False,False,True)
+        waiting = {}
+        SHARE = (512,512,352,256)
+        CV_S = (False,False,True,True)
         OUT_S = (False,False,True,False,True)
         TURN_BANK = (6, 7, 0, 1)
         for b in range(BLOCKS):
@@ -189,15 +195,15 @@ def tile_attend_tab_timestable_twostores_kernel(
             gather_split(picked[:], first_pool[b], list1, SHARE[b])
             turned = banks.tile([P, 2, P], F32, name="turned1_%d" % b, tag="bank%d" % TURN_BANK[b])
             turn(picked, turned)
-            if last:
-                waiting(tag="picked1_%d" % b)
-            woven = held.tile([P, P * PACK], BF16, name="first_woven%d" % b, tag="vals_3" if b == 2 else "first_woven%d" % b, align_bytes=64)
+            if b in waiting:
+                waiting[b](tag="picked1_%d" % b)
+            woven = held.tile([P, P * PACK], BF16, name="first_woven%d" % b, align_bytes=64)
             copy_out(
                 CV_S[b],
                 woven[:].bitcast(F32).rearrange("p (e u) -> p e u", u=2),
                 turned[:].rearrange("p u e -> p e u"),
             )
-            first = quantize(woven[:], P, "first%d" % b, "vals_%d" % (b + 1) if b < 2 else None)
+            first = quantize(woven[:], P, "first%d" % b, None if last else "vals_%d" % (b + 1))
             pieces = 2 if last else 1
             width = J // pieces
             for h in range(pieces):
@@ -221,7 +227,7 @@ def tile_attend_tab_timestable_twostores_kernel(
                     copy_out(OUT_S[b + h], result[:], acc[:])
                     nc.sync.dma_start(out=out[P * b : P * (b + 1), cols], in_=result[:])
 
-                if b == 1:
-                    waiting = leave
+                if b < 2:
+                    waiting[b + 2] = leave
                 else:
                     leave()

@@ -18,7 +18,18 @@ COPY = mybir.ActivationFunctionType.Copy
 
 P = 128
 PACK = 4
+LISTED = 512
+PER_COLUMN = 16
 BLOCKS = E // P
+QUADRANT = 32
+
+NOTES_ON_SCALAR = (LISTED, 0, 0, 352)
+GIVEN_ON_SCALAR = (256, LISTED, LISTED, LISTED)
+FIRST_ON_SCALAR = (LISTED, 384, 320, 256)
+NOTES_WOVEN_ON_SCALAR = 256
+
+SECOND_BANKS = (4, 5)
+FIRST_BANKS = (6, 7, 0, 1)
 
 
 def tile_attend_tab_timestable_twostores_kernel(
@@ -30,58 +41,76 @@ def tile_attend_tab_timestable_twostores_kernel(
         banks = ctx.enter_context(tc.psum_pool(name="banks", bufs=1))
 
         def load_list(src, name):
-            t = held.tile([P, I // 16], U16, name=name)
-            nc.sync.dma_start(t[:], src)
-            return t
+            offsets = held.tile([P, LISTED // PER_COLUMN], U16, name=name)
+            nc.sync.dma_start(offsets[:], src)
+            return offsets
 
         def load(src, width, dtype, name):
-            t = held.tile([P, width], dtype, name=name, align_bytes=64)
-            nc.sync.dma_start(out=t[:], in_=src)
-            return t
+            loaded = held.tile([P, width], dtype, name=name, align_bytes=64)
+            nc.sync.dma_start(out=loaded[:], in_=src)
+            return loaded
 
-        def gather(on_scalar, dst, window, offsets):
-            if on_scalar:
-                nc.scalar.activation(dst, window[:].indirect(offsets), COPY)
-            else:
-                nc.vector.tensor_copy(dst, window[:].indirect(offsets))
-
-        def interleave(planes, name, cut=0):
-            woven = held.tile([P, J, PACK], BF16, name=name, align_bytes=64)
-            if cut > 0:
-                nc.scalar.copy(
-                    out=woven[:, 0:cut, :].rearrange("p (c n) t -> p c t n", n=4),
-                    in_=planes[:, :, 0:cut].rearrange("p t (c n) -> p c t n", n=4),
+        def gather(dst, window, offsets, on_scalar):
+            cut = on_scalar // PER_COLUMN
+            if on_scalar > 0:
+                nc.scalar.activation(dst[:, 0:on_scalar], window[:].indirect(offsets[:, 0:cut]), COPY)
+            if on_scalar < LISTED:
+                nc.vector.tensor_copy(
+                    dst[:, on_scalar:LISTED], window[:].indirect(offsets[:, cut : LISTED // PER_COLUMN])
                 )
-            nc.vector.tensor_copy(
-                out=woven[:, cut:J, :].rearrange("p (c n) t -> p c t n", n=4),
-                in_=planes[:, :, cut:J].rearrange("p t (c n) -> p c t n", n=4),
-            )
+
+        def copy(on_scalar, dst, src):
+            if on_scalar:
+                nc.scalar.copy(out=dst, in_=src)
+            else:
+                nc.vector.tensor_copy(out=dst, in_=src)
+
+        def weave(planes, name, columns_on_scalar):
+            woven = held.tile([P, J, PACK], BF16, name=name, align_bytes=64)
+            for on_scalar, lo, hi in ((True, 0, columns_on_scalar), (False, columns_on_scalar, J)):
+                if hi > lo:
+                    copy(
+                        on_scalar,
+                        woven[:, lo:hi, :].rearrange("p (c n) t -> p c t n", n=4),
+                        planes[:, :, lo:hi].rearrange("p t (c n) -> p c t n", n=4),
+                    )
             return woven[:].rearrange("p j t -> p (j t)")
 
-        def quantize(src, width, name, tag=None):
-            codes = held.tile([P, width], U32, name=name + "_codes", tag=tag or name + "_codes", align_bytes=64)
+        def quantize(src, width, name, codes_tag):
+            codes = held.tile([P, width], U32, name=name + "_codes", tag=codes_tag, align_bytes=64)
             scales = held.tile([P, width], U8, name=name + "_scales", align_bytes=64)
             nc.vector.quantize_mx(out=codes[:].bitcast(FP8X4), scales=scales[:], in_=src)
             return codes, scales
+
+        def multiply(acc, stationary, moving, start, stop):
+            nc.tensor.matmul_mx(
+                out=acc,
+                lhsT=stationary[0].bitcast(FP8X4),
+                lhsT_scale=stationary[1],
+                rhs=moving[0].bitcast(FP8X4),
+                rhs_scale=moving[1],
+                start=start,
+                stop=stop,
+            )
 
         key_scales = held.tile([P, T], U8, name="key_scales")
         nc.gpsimd.memset(key_scales[:].bitcast(I32), 0)
         factors = []
         for s, src in enumerate((rowf, rowf2)):
-            t = held.tile([P, PACK], F32, name="factor%d" % s)
-            nc.gpsimd.dma_start(out=t[:], in_=src.rearrange("(p t) o -> p (t o)", t=PACK))
-            factors.append(t)
+            factor = held.tile([P, PACK], F32, name="factor%d" % s)
+            nc.gpsimd.dma_start(out=factor[:], in_=src.rearrange("(p t) o -> p (t o)", t=PACK))
+            factors.append(factor)
         ident = held.tile([P, P], F32, name="ident")
         make_identity(nc, ident[:])
 
-        notes_rows = notes.rearrange("(p t) u -> p t u", t=PACK)
-        given_rows = given.rearrange("(p t) z -> p t z", t=PACK)
         def load_scale_rows(q):
             nc.sync.dma_start(
-                out=key_scales[32 * q : 32 * q + 4, :].bitcast(I32),
+                out=key_scales[QUADRANT * q : QUADRANT * q + 4, :].bitcast(I32),
                 in_=keys_scales[0, 4 * q : 4 * q + 4, :].bitcast(I32),
             )
 
+        notes_rows = notes.rearrange("(p t) u -> p t u", t=PACK)
+        given_rows = given.rearrange("(p t) z -> p t z", t=PACK)
         note_pool = [load(notes_rows[:, 0, :], U, F32, "notes0")]
         list2 = load_list(offs2, "list2")
         note_pool.append(load(notes_rows[:, 1, :], U, F32, "notes1"))
@@ -92,40 +121,23 @@ def tile_attend_tab_timestable_twostores_kernel(
         note_pool.append(load(notes_rows[:, 3, :], U, F32, "notes3"))
         load_scale_rows(2)
         load_scale_rows(3)
-
-        def load_second(b):
-            return load(vals2[P * b : P * (b + 1), :], Y, F32, "vals2_%d" % b)
-
-        EARLY = 0
-        second_pool = [load_second(b) for b in range(EARLY)]
         key_words = load(keys_words[0].rearrange("p n t -> p (n t)").bitcast(I32), T, I32, "key_words")
         list3 = load_list(offs3, "list3")
         given_pool = [load(given_rows[:, t, :], Z, F32, "given%d" % t) for t in range(PACK)]
         list4 = load_list(offs4, "list4")
-        second_pool.extend(load_second(b) for b in range(EARLY, BLOCKS))
+        second_pool = [load(vals2[P * b : P * (b + 1), :], Y, F32, "vals2_%d" % b) for b in range(BLOCKS)]
         first_pool = [load(vals[P * b : P * (b + 1), :], T, F32, "vals_%d" % b) for b in range(BLOCKS)]
 
-        def gather_split(dst, window, offsets, cut):
-            if cut > 0:
-                gather(True, dst[:, 0:cut], window, offsets[:, 0 : cut // 16])
-            if cut < I:
-                gather(False, dst[:, cut:I], window, offsets[:, cut // 16 : I // 16])
-
-        def copy_out(on_scalar, dst, src):
-            if on_scalar:
-                nc.scalar.copy(out=dst, in_=src)
-            else:
-                nc.vector.tensor_copy(out=dst, in_=src)
-
         note_planes = held.tile([P, PACK, J], BF16, name="note_planes")
-        NOTE_S = (512,0,0,352)
         for t in range(PACK):
-            gather_split(note_planes[:, t, :], note_pool[t], list2, NOTE_S[t])
+            gather(note_planes[:, t, :], note_pool[t], list2, NOTES_ON_SCALAR[t])
         picked_scales = held.tile([P, I], U8, name="picked_scales", align_bytes=64)
         nc.vector.tensor_copy(
             picked_scales[:].rearrange("p (r s) -> p s r", r=PACK), key_scales[:].indirect(list1[:])
         )
-        note_codes, note_scales = quantize(interleave(note_planes, "note_woven", 256), J, "note")
+        note_codes, note_scales = quantize(
+            weave(note_planes, "note_woven", NOTES_WOVEN_ON_SCALAR), J, "note", "note_codes"
+        )
         picked_words = held.tile([P, I], U32, name="picked_words", align_bytes=64)
         nc.vector.tensor_copy(
             picked_words[:].rearrange("p (r s) -> p s r", r=PACK), key_words[:].bitcast(U32).indirect(list1[:])
@@ -133,101 +145,82 @@ def tile_attend_tab_timestable_twostores_kernel(
 
         table_planes = [held.tile([P, PACK, J], BF16, name="table_planes%d" % s) for s in range(2)]
         for r in range(PACK):
-            cols = slice(P * r, P * (r + 1))
-            g1 = banks.tile([P, J], F32, name="g1_%d" % r, tag="bank%d" % r)
-            nc.tensor.matmul_mx(
-                out=g1[:],
-                lhsT=picked_words[:, cols].bitcast(FP8X4),
-                lhsT_scale=picked_scales[:, cols],
-                rhs=note_codes[:].bitcast(FP8X4),
-                rhs_scale=note_scales[:],
-                start=True,
-                stop=True,
+            rows = slice(P * r, P * (r + 1))
+            scores = banks.tile([P, J], F32, name="scores%d" % r, tag="bank%d" % r)
+            multiply(
+                scores[:], (picked_words[:, rows], picked_scales[:, rows]), (note_codes[:], note_scales[:]), True, True
             )
             picked_given = held.tile([P, J], F32, name="picked_given%d" % r)
-            gather_split(picked_given[:], given_pool[r], list3, (256,512,512,512)[r])
+            gather(picked_given[:], given_pool[r], list3, GIVEN_ON_SCALAR[r])
             for s in range(2):
                 nc.vector.scalar_tensor_tensor(
                     out=table_planes[s][:, r, :],
-                    in0=g1[:],
+                    in0=scores[:],
                     scalar=factors[s][:, r : r + 1],
                     in1=picked_given[:],
                     op0=MULT,
                     op1=MULT,
                 )
-        tables = [quantize(interleave(table_planes[s], "table_woven%d" % s), J, "table%d" % s) for s in range(2)]
+        first_table, second_table = [
+            quantize(weave(table_planes[s], "table_woven%d" % s, 0), J, "table%d" % s, "table%d_codes" % s)
+            for s in range(2)
+        ]
 
         def turn(picked, turned):
             words = picked[:].bitcast(F32)
             for u in range(2):
                 nc.tensor.transpose(turned[:, u, :], words[:, u : I // 2 : 2], ident[:])
 
-        second = {}
-
-        def second_group(blocks, bank, on_scalar):
-            n = len(blocks)
-            woven = held.tile([P, n * P * PACK], BF16, name="second_woven%d" % blocks[0], align_bytes=64)
-            turned = banks.tile([P, n, 2, P], F32, name="turned2_%d" % blocks[0], tag="bank%d" % bank)
-            for k, b in enumerate(blocks):
-                picked = held.tile([P, I], BF16, name="picked2_%d" % b)
-                gather(True, picked[:], second_pool[b], list4[:])
+        second = []
+        for pair, bank in enumerate(SECOND_BANKS):
+            later = pair == 1
+            woven_tag = "vals_0" if later else "second_woven"
+            woven = held.tile([P, 2 * P * PACK], BF16, name="second_woven%d" % pair, tag=woven_tag, align_bytes=64)
+            turned = banks.tile([P, 2, 2, P], F32, name="second_turned%d" % pair, tag="bank%d" % bank)
+            for k in range(2):
+                picked = held.tile([P, I], BF16, name="second_picked%d" % (2 * pair + k))
+                gather(picked[:], second_pool[2 * pair + k], list4, LISTED)
                 turn(picked, turned[:, k])
-            copy_out(
-                on_scalar,
-                woven[:].bitcast(F32).rearrange("p (k e u) -> p k e u", k=n, u=2),
+            copy(
+                later,
+                woven[:].bitcast(F32).rearrange("p (k e u) -> p k e u", k=2, u=2),
                 turned[:].rearrange("p k u e -> p k e u"),
             )
-            codes, scales = quantize(woven[:], n * P, "second%d" % blocks[0])
-            for k, b in enumerate(blocks):
-                second[b] = (codes[:, P * k : P * (k + 1)], scales[:, P * k : P * (k + 1)])
+            codes, scales = quantize(woven[:], 2 * P, "second%d" % pair, "second%d_codes" % pair)
+            for k in range(2):
+                second.append((codes[:, P * k : P * (k + 1)], scales[:, P * k : P * (k + 1)]))
 
-        for blocks, bank, on_scalar in (((0,1),4,False),((2,3),5,False)):
-            second_group(blocks, bank, on_scalar)
+        def store(acc, b, cols, on_scalar, name, tag):
+            result = held.tile([P, cols.stop - cols.start], F32, name=name, tag=tag, align_bytes=64)
+            copy(on_scalar, result[:], acc[:])
+            nc.sync.dma_start(out=out[P * b : P * (b + 1), cols], in_=result[:])
 
-        waiting = {}
-        SHARE = (512,512,352,256)
-        CV_S = (False,False,True,True)
-        OUT_S = (False,False,True,False,True)
-        TURN_BANK = (6, 7, 0, 1)
+        sums = []
         for b in range(BLOCKS):
             last = b == BLOCKS - 1
-            picked = held.tile([P, I], BF16, name="picked1_%d" % b, align_bytes=64)
-            gather_split(picked[:], first_pool[b], list1, SHARE[b])
-            turned = banks.tile([P, 2, P], F32, name="turned1_%d" % b, tag="bank%d" % TURN_BANK[b])
+            picked_tag = "first_picked%d" % b
+            picked = held.tile([P, I], BF16, name=picked_tag, align_bytes=64)
+            gather(picked[:], first_pool[b], list1, FIRST_ON_SCALAR[b])
+            turned = banks.tile([P, 2, P], F32, name="first_turned%d" % b, tag="bank%d" % FIRST_BANKS[b])
             turn(picked, turned)
-            if b in waiting:
-                waiting[b](tag="picked1_%d" % b)
+            if b >= 2:
+                store(sums[b - 2], b - 2, slice(0, J), False, "result%d" % (b - 2), picked_tag)
             woven = held.tile([P, P * PACK], BF16, name="first_woven%d" % b, align_bytes=64)
-            copy_out(
-                CV_S[b],
+            copy(
+                b >= 2,
                 woven[:].bitcast(F32).rearrange("p (e u) -> p e u", u=2),
                 turned[:].rearrange("p u e -> p e u"),
             )
-            first = quantize(woven[:], P, "first%d" % b, None if last else "vals_%d" % (b + 1))
-            pieces = 2 if last else 1
-            width = J // pieces
-            for h in range(pieces):
+            codes, scales = quantize(woven[:], P, "first%d" % b, "first_last_codes" if last else "vals_%d" % (b + 1))
+            halves = 2 if last else 1
+            width = J // halves
+            for h in range(halves):
                 cols = slice(width * h, width * (h + 1))
-                acc = banks.tile([P, width], F32, name="acc%d_%d" % (b, h), tag="bank%d" % (TURN_BANK[b] if h == 0 else 6))
-                passes = [(second[b][0], second[b][1], tables[1]), (first[0][:], first[1][:], tables[0])]
-                if (False,False,False,False,False)[b + h]:
-                    passes = passes[::-1]
-                for n, (codes, scales, table) in enumerate(passes):
-                    nc.tensor.matmul_mx(
-                        out=acc[:],
-                        lhsT=codes.bitcast(FP8X4),
-                        lhsT_scale=scales,
-                        rhs=table[0][:, cols].bitcast(FP8X4),
-                        rhs_scale=table[1][:, cols],
-                        start=(n == 0),
-                        stop=(n == 1),
-                    )
-                def leave(b=b, h=h, acc=acc, cols=cols, width=width, tag=None):
-                    result = held.tile([P, width], F32, name="result%d_%d" % (b, h), tag=tag or "result%d_%d" % (b, h), align_bytes=64)
-                    copy_out(OUT_S[b + h], result[:], acc[:])
-                    nc.sync.dma_start(out=out[P * b : P * (b + 1), cols], in_=result[:])
-
-                if b < 2:
-                    waiting[b + 2] = leave
-                else:
-                    leave()
+                bank = FIRST_BANKS[b] if h == 0 else FIRST_BANKS[0]
+                acc = banks.tile([P, width], F32, name="acc%d_%d" % (b, h), tag="bank%d" % bank)
+                multiply(acc[:], second[b], (second_table[0][:, cols], second_table[1][:, cols]), True, False)
+                multiply(acc[:], (codes[:], scales[:]), (first_table[0][:, cols], first_table[1][:, cols]), False, True)
+                sums.append(acc)
+                if b >= 2:
+                    name = "result%d_%d" % (b, h)
+                    store(acc, b, cols, not last or h == 1, name, name)

from contextlib import ExitStack

import concourse.mybir as mybir
from concourse.masks import make_identity

D, T, I, J, U, Z, E, Y = 512, 2048, 512, 512, 1024, 1024, 512, 1024
FLOPS = 2 * D * I * J + 2 * 2 * I * E * J

F32 = mybir.dt.float32
BF16 = mybir.dt.bfloat16
I32 = mybir.dt.int32
U32 = mybir.dt.uint32
U16 = mybir.dt.uint16
U8 = mybir.dt.uint8
FP8X4 = mybir.dt.float8_e4m3fn_x4
MULT = mybir.AluOpType.mult
COPY = mybir.ActivationFunctionType.Copy

P = 128
PACK = 4
LISTED = 512
PER_COLUMN = 16
BLOCKS = E // P
QUADRANT = 32

NOTES_ON_SCALAR = (LISTED, 0, 0, 352)
GIVEN_ON_SCALAR = (256, LISTED, LISTED, LISTED)
FIRST_ON_SCALAR = (LISTED, 384, 320, 256)
NOTES_WOVEN_ON_SCALAR = 256

SECOND_BANKS = (4, 5)
FIRST_BANKS = (6, 7, 0, 1)


def tile_attend_tab_timestable_twostores_kernel(
    tc, keys_words, keys_scales, notes, given, rowf, rowf2, vals, vals2, offs, offs2, offs3, offs4, out
):
    nc = tc.nc
    with ExitStack() as ctx:
        held = ctx.enter_context(tc.tile_pool(name="held", bufs=1))
        banks = ctx.enter_context(tc.psum_pool(name="banks", bufs=1))

        def load_list(src, name):
            offsets = held.tile([P, LISTED // PER_COLUMN], U16, name=name)
            nc.sync.dma_start(offsets[:], src)
            return offsets

        def load(src, width, dtype, name):
            loaded = held.tile([P, width], dtype, name=name, align_bytes=64)
            nc.sync.dma_start(out=loaded[:], in_=src)
            return loaded

        def gather(dst, window, offsets, on_scalar):
            cut = on_scalar // PER_COLUMN
            if on_scalar > 0:
                nc.scalar.activation(dst[:, 0:on_scalar], window[:].indirect(offsets[:, 0:cut]), COPY)
            if on_scalar < LISTED:
                nc.vector.tensor_copy(
                    dst[:, on_scalar:LISTED], window[:].indirect(offsets[:, cut : LISTED // PER_COLUMN])
                )

        def copy(on_scalar, dst, src):
            if on_scalar:
                nc.scalar.copy(out=dst, in_=src)
            else:
                nc.vector.tensor_copy(out=dst, in_=src)

        def weave(planes, name, columns_on_scalar):
            woven = held.tile([P, J, PACK], BF16, name=name, align_bytes=64)
            for on_scalar, lo, hi in ((True, 0, columns_on_scalar), (False, columns_on_scalar, J)):
                if hi > lo:
                    copy(
                        on_scalar,
                        woven[:, lo:hi, :].rearrange("p (c n) t -> p c t n", n=4),
                        planes[:, :, lo:hi].rearrange("p t (c n) -> p c t n", n=4),
                    )
            return woven[:].rearrange("p j t -> p (j t)")

        def quantize(src, width, name, codes_tag):
            codes = held.tile([P, width], U32, name=name + "_codes", tag=codes_tag, align_bytes=64)
            scales = held.tile([P, width], U8, name=name + "_scales", align_bytes=64)
            nc.vector.quantize_mx(out=codes[:].bitcast(FP8X4), scales=scales[:], in_=src)
            return codes, scales

        def multiply(acc, stationary, moving, start, stop):
            nc.tensor.matmul_mx(
                out=acc,
                lhsT=stationary[0].bitcast(FP8X4),
                lhsT_scale=stationary[1],
                rhs=moving[0].bitcast(FP8X4),
                rhs_scale=moving[1],
                start=start,
                stop=stop,
            )

        key_scales = held.tile([P, T], U8, name="key_scales")
        nc.gpsimd.memset(key_scales[:].bitcast(I32), 0)
        factors = []
        for s, src in enumerate((rowf, rowf2)):
            factor = held.tile([P, PACK], F32, name="factor%d" % s)
            nc.gpsimd.dma_start(out=factor[:], in_=src.rearrange("(p t) o -> p (t o)", t=PACK))
            factors.append(factor)
        ident = held.tile([P, P], F32, name="ident")
        make_identity(nc, ident[:])

        def load_scale_rows(q):
            nc.sync.dma_start(
                out=key_scales[QUADRANT * q : QUADRANT * q + 4, :].bitcast(I32),
                in_=keys_scales[0, 4 * q : 4 * q + 4, :].bitcast(I32),
            )

        notes_rows = notes.rearrange("(p t) u -> p t u", t=PACK)
        given_rows = given.rearrange("(p t) z -> p t z", t=PACK)
        note_pool = [load(notes_rows[:, 0, :], U, F32, "notes0")]
        list2 = load_list(offs2, "list2")
        note_pool.append(load(notes_rows[:, 1, :], U, F32, "notes1"))
        list1 = load_list(offs, "list1")
        note_pool.append(load(notes_rows[:, 2, :], U, F32, "notes2"))
        load_scale_rows(0)
        load_scale_rows(1)
        note_pool.append(load(notes_rows[:, 3, :], U, F32, "notes3"))
        load_scale_rows(2)
        load_scale_rows(3)
        key_words = load(keys_words[0].rearrange("p n t -> p (n t)").bitcast(I32), T, I32, "key_words")
        list3 = load_list(offs3, "list3")
        given_pool = [load(given_rows[:, t, :], Z, F32, "given%d" % t) for t in range(PACK)]
        list4 = load_list(offs4, "list4")
        second_pool = [load(vals2[P * b : P * (b + 1), :], Y, F32, "vals2_%d" % b) for b in range(BLOCKS)]
        first_pool = [load(vals[P * b : P * (b + 1), :], T, F32, "vals_%d" % b) for b in range(BLOCKS)]

        note_planes = held.tile([P, PACK, J], BF16, name="note_planes")
        for t in range(PACK):
            gather(note_planes[:, t, :], note_pool[t], list2, NOTES_ON_SCALAR[t])
        picked_scales = held.tile([P, I], U8, name="picked_scales", align_bytes=64)
        nc.vector.tensor_copy(
            picked_scales[:].rearrange("p (r s) -> p s r", r=PACK), key_scales[:].indirect(list1[:])
        )
        note_codes, note_scales = quantize(
            weave(note_planes, "note_woven", NOTES_WOVEN_ON_SCALAR), J, "note", "note_codes"
        )
        picked_words = held.tile([P, I], U32, name="picked_words", align_bytes=64)
        nc.vector.tensor_copy(
            picked_words[:].rearrange("p (r s) -> p s r", r=PACK), key_words[:].bitcast(U32).indirect(list1[:])
        )

        table_planes = [held.tile([P, PACK, J], BF16, name="table_planes%d" % s) for s in range(2)]
        for r in range(PACK):
            rows = slice(P * r, P * (r + 1))
            scores = banks.tile([P, J], F32, name="scores%d" % r, tag="bank%d" % r)
            multiply(
                scores[:], (picked_words[:, rows], picked_scales[:, rows]), (note_codes[:], note_scales[:]), True, True
            )
            picked_given = held.tile([P, J], F32, name="picked_given%d" % r)
            gather(picked_given[:], given_pool[r], list3, GIVEN_ON_SCALAR[r])
            for s in range(2):
                nc.vector.scalar_tensor_tensor(
                    out=table_planes[s][:, r, :],
                    in0=scores[:],
                    scalar=factors[s][:, r : r + 1],
                    in1=picked_given[:],
                    op0=MULT,
                    op1=MULT,
                )
        first_table, second_table = [
            quantize(weave(table_planes[s], "table_woven%d" % s, 0), J, "table%d" % s, "table%d_codes" % s)
            for s in range(2)
        ]

        def turn(picked, turned):
            words = picked[:].bitcast(F32)
            for u in range(2):
                nc.tensor.transpose(turned[:, u, :], words[:, u : I // 2 : 2], ident[:])

        second = []
        for pair, bank in enumerate(SECOND_BANKS):
            later = pair == 1
            woven_tag = "vals_0" if later else "second_woven"
            woven = held.tile([P, 2 * P * PACK], BF16, name="second_woven%d" % pair, tag=woven_tag, align_bytes=64)
            turned = banks.tile([P, 2, 2, P], F32, name="second_turned%d" % pair, tag="bank%d" % bank)
            for k in range(2):
                picked = held.tile([P, I], BF16, name="second_picked%d" % (2 * pair + k))
                gather(picked[:], second_pool[2 * pair + k], list4, LISTED)
                turn(picked, turned[:, k])
            copy(
                later,
                woven[:].bitcast(F32).rearrange("p (k e u) -> p k e u", k=2, u=2),
                turned[:].rearrange("p k u e -> p k e u"),
            )
            codes, scales = quantize(woven[:], 2 * P, "second%d" % pair, "second%d_codes" % pair)
            for k in range(2):
                second.append((codes[:, P * k : P * (k + 1)], scales[:, P * k : P * (k + 1)]))

        def store(acc, b, cols, on_scalar, name, tag):
            result = held.tile([P, cols.stop - cols.start], F32, name=name, tag=tag, align_bytes=64)
            copy(on_scalar, result[:], acc[:])
            nc.sync.dma_start(out=out[P * b : P * (b + 1), cols], in_=result[:])

        sums = []
        for b in range(BLOCKS):
            last = b == BLOCKS - 1
            picked_tag = "first_picked%d" % b
            picked = held.tile([P, I], BF16, name=picked_tag, align_bytes=64)
            gather(picked[:], first_pool[b], list1, FIRST_ON_SCALAR[b])
            turned = banks.tile([P, 2, P], F32, name="first_turned%d" % b, tag="bank%d" % FIRST_BANKS[b])
            turn(picked, turned)
            if b >= 2:
                store(sums[b - 2], b - 2, slice(0, J), False, "result%d" % (b - 2), picked_tag)
            woven = held.tile([P, P * PACK], BF16, name="first_woven%d" % b, align_bytes=64)
            copy(
                b >= 2,
                woven[:].bitcast(F32).rearrange("p (e u) -> p e u", u=2),
                turned[:].rearrange("p u e -> p e u"),
            )
            codes, scales = quantize(woven[:], P, "first%d" % b, "first_last_codes" if last else "vals_%d" % (b + 1))
            halves = 2 if last else 1
            width = J // halves
            for h in range(halves):
                cols = slice(width * h, width * (h + 1))
                bank = FIRST_BANKS[b] if h == 0 else FIRST_BANKS[0]
                acc = banks.tile([P, width], F32, name="acc%d_%d" % (b, h), tag="bank%d" % bank)
                multiply(acc[:], second[b], (second_table[0][:, cols], second_table[1][:, cols]), True, False)
                multiply(acc[:], (codes[:], scales[:]), (first_table[0][:, cols], first_table[1][:, cols]), False, True)
                sums.append(acc)
                if b >= 2:
                    name = "result%d_%d" % (b, h)
                    store(acc, b, cols, not last or h == 1, name, name)
